import numpy as np
import ml_dtypes

BF16 = ml_dtypes.bfloat16


def bf(x):
    return np.asarray(x, np.float32).astype(BF16)


def f32(x):
    return np.asarray(x, np.float32)


def f64(x):
    return np.asarray(x).astype(np.float64)


def striped(idx):
    return np.tile(idx.reshape(-1, 16).T, (8, 1))


S, K, M, N, E, Q = 256, 128, 512, 192, 2, 96


def setup_inputs():
    return {"base": bf(np.random.standard_normal((M, S))), "x": bf(np.random.standard_normal((K, N))), "w": bf(np.random.standard_normal((E, K, M)) / np.sqrt(K)), "b": f32(0.5 * np.random.standard_normal((M, 1))), "offs": striped(np.random.permutation(S)[:N])}


def reference(base, x, w, b, offs):
    idx = offs[:16].T.reshape(-1)
    z = f64(base).copy()
    for e in range(E):
        z[:, idx[e * Q : (e + 1) * Q]] = f64(w)[e].T @ f64(x)[:, e * Q : (e + 1) * Q]
    return z + f64(b)

@@ -1,0 +1,65 @@
+import concourse.mybir as mybir
+from concourse.masks import make_identity
+
+BF16, F32, U16 = mybir.dt.bfloat16, mybir.dt.float32, mybir.dt.uint16
+
+P = 128
+TOKENS = 256
+FEATURES = 512
+BLOCKS = FEATURES // P
+EXPERTS = 2
+PIECE = 96
+ENTRIES = EXPERTS * PIECE
+PIECE_COLS = PIECE // 16
+
+FLOPS = 2 * P * FEATURES * ENTRIES
+
+
+def tile_scatter_matmul_kernel(tc, base, x, w, b, offs, out):
+    nc = tc.nc
+    with (
+        tc.tile_pool(name="held", bufs=1) as held,
+        tc.tile_pool(name="results", bufs=BLOCKS) as results,
+        tc.psum_pool(name="windows", bufs=1) as windows,
+    ):
+        offsets = held.tile([P, ENTRIES // 16], U16, name="offsets")
+        nc.sync.dma_start(offsets[:], offs)
+        base_sb = held.tile([P, BLOCKS, TOKENS], BF16, name="base_sb")
+        nc.scalar.dma_start(base_sb[:], base.rearrange("(a p) t -> p a t", p=P))
+        w_sb = held.tile([P, EXPERTS, FEATURES], BF16, name="w_sb")
+        nc.sync.dma_start(w_sb[:], w.rearrange("e k m -> k e m"))
+        x_sb = held.tile([P, ENTRIES], BF16, name="x_sb")
+        nc.scalar.dma_start(x_sb[:], x)
+        bias_sb = held.tile([P, BLOCKS], F32, name="bias_sb")
+        with nc.allow_non_contiguous_dma(reason="one float32 bias value to a partition"):
+            nc.gpsimd.dma_start(bias_sb[:], b.rearrange("(a p) o -> p (a o)", p=P))
+
+        ident = held.tile([P, P], BF16, name="ident")
+        make_identity(nc, ident[:])
+
+        window = [windows.tile([P, TOKENS], F32, name="window%d" % a) for a in range(BLOCKS)]
+        for a in range(BLOCKS):
+            nc.tensor.matmul(window[a][:], ident[:], base_sb[:, a, :], start=True, stop=True)
+
+        for a in range(BLOCKS):
+            for e in range(EXPERTS):
+                nc.tensor.matmul(
+                    window[a][:].indirect(offsets[:, e * PIECE_COLS : (e + 1) * PIECE_COLS]),
+                    w_sb[:, e, a * P : (a + 1) * P],
+                    x_sb[:, e * PIECE : (e + 1) * PIECE],
+                    start=True,
+                    stop=True,
+                )
+            result = results.tile([P, TOKENS], F32, name="result")
+            if a % 2 == 0:
+                nc.vector.tensor_scalar(
+                    out=result[:], in0=window[a][:], scalar1=bias_sb[:, a : a + 1],
+                    scalar2=None, op0=mybir.AluOpType.add,
+                )
+                nc.sync.dma_start(out[a * P : (a + 1) * P, :], result[:])
+            else:
+                nc.scalar.activation(
+                    out=result[:], in_=window[a][:],
+                    func=mybir.ActivationFunctionType.Identity, bias=bias_sb[:, a : a + 1],
+                )
+                nc.scalar.dma_start(out[a * P : (a + 1) * P, :], result[:])

@@ -22,30 +22,39 @@ def tile_scatter_matmul_kernel(tc, base, x, w, b, offs, out):
         tc.tile_pool(name="results", bufs=BLOCKS) as results,
         tc.psum_pool(name="windows", bufs=1) as windows,
     ):
-        offsets = held.tile([P, ENTRIES // 16], U16, name="offsets")
-        nc.sync.dma_start(offsets[:], offs)
-        base_sb = held.tile([P, BLOCKS, TOKENS], BF16, name="base_sb")
-        nc.scalar.dma_start(base_sb[:], base.rearrange("(a p) t -> p a t", p=P))
-        w_sb = held.tile([P, EXPERTS, FEATURES], BF16, name="w_sb")
-        nc.sync.dma_start(w_sb[:], w.rearrange("e k m -> k e m"))
-        x_sb = held.tile([P, ENTRIES], BF16, name="x_sb")
-        nc.scalar.dma_start(x_sb[:], x)
-        bias_sb = held.tile([P, BLOCKS], F32, name="bias_sb")
-        with nc.allow_non_contiguous_dma(reason="one float32 bias value to a partition"):
-            nc.gpsimd.dma_start(bias_sb[:], b.rearrange("(a p) o -> p (a o)", p=P))
-
         ident = held.tile([P, P], BF16, name="ident")
         make_identity(nc, ident[:])
 
+        queues = [nc.sync, nc.scalar]
+        base_sb = [held.tile([P, 2, TOKENS], BF16, name="base_sb%d" % h) for h in range(2)]
+        for h in range(2):
+            queues[h].dma_start(
+                base_sb[h][:], base[h * 2 * P : (h + 1) * 2 * P, :].rearrange("(a p) t -> p a t", p=P)
+            )
+        offsets = held.tile([P, ENTRIES // 16], U16, name="offsets")
+        nc.sync.dma_start(offsets[:], offs)
+        x_sb = held.tile([P, ENTRIES], BF16, name="x_sb")
+        nc.scalar.dma_start(x_sb[:], x)
+        w_sb = [held.tile([P, FEATURES], BF16, name="w_sb%d" % e) for e in range(EXPERTS)]
+        for e in range(EXPERTS):
+            queues[e].dma_start(w_sb[e][:], w[e])
+        bias_sb = held.tile([P, BLOCKS], F32, name="bias_sb")
+        with nc.allow_non_contiguous_dma(reason="one float32 bias value to a partition"):
+            nc.sync.dma_start(bias_sb[:], b.rearrange("(a p) o -> p (a o)", p=P))
+
+        scratch = held.tile([P, 1], F32, name="scratch")
+        nc.vector.memset(scratch[:], 0.0)
+        nc.scalar.activation(out=scratch[:], in_=scratch[:], func=mybir.ActivationFunctionType.Identity)
+
         window = [windows.tile([P, TOKENS], F32, name="window%d" % a) for a in range(BLOCKS)]
         for a in range(BLOCKS):
-            nc.tensor.matmul(window[a][:], ident[:], base_sb[:, a, :], start=True, stop=True)
+            nc.tensor.matmul(window[a][:], ident[:], base_sb[a // 2][:, a % 2, :], start=True, stop=True)
 
         for a in range(BLOCKS):
             for e in range(EXPERTS):
                 nc.tensor.matmul(
                     window[a][:].indirect(offsets[:, e * PIECE_COLS : (e + 1) * PIECE_COLS]),
-                    w_sb[:, e, a * P : (a + 1) * P],
+                    w_sb[e][:, a * P : (a + 1) * P],
                     x_sb[:, e * PIECE : (e + 1) * PIECE],
                     start=True,
                     stop=True,

@@ -12,6 +12,8 @@ PIECE = 96
 ENTRIES = EXPERTS * PIECE
 PIECE_COLS = PIECE // 16
 
+WARM_MATMULS = 8
+
 FLOPS = 2 * P * FEATURES * ENTRIES
 
 
@@ -22,6 +24,12 @@ def tile_scatter_matmul_kernel(tc, base, x, w, b, offs, out):
         tc.tile_pool(name="results", bufs=BLOCKS) as results,
         tc.psum_pool(name="windows", bufs=1) as windows,
     ):
+        zeros = held.tile([P, TOKENS], BF16, name="zeros")
+        nc.gpsimd.memset(zeros[:], 0.0)
+        idle_bank = windows.tile([P, TOKENS], F32, name="idle_bank")
+        for i in range(WARM_MATMULS):
+            nc.tensor.matmul(idle_bank[:], zeros[:, 0:P], zeros[:], start=True, stop=True)
+
         ident = held.tile([P, P], BF16, name="ident")
         make_identity(nc, ident[:])
 

@@ -12,7 +12,7 @@ PIECE = 96
 ENTRIES = EXPERTS * PIECE
 PIECE_COLS = PIECE // 16
 
-WARM_MATMULS = 8
+WARM_MATMULS = 5
 
 FLOPS = 2 * P * FEATURES * ENTRIES
 

@@ -37,7 +37,8 @@ def tile_scatter_matmul_kernel(tc, base, x, w, b, offs, out):
         base_sb = [held.tile([P, 2, TOKENS], BF16, name="base_sb%d" % h) for h in range(2)]
         for h in range(2):
             queues[h].dma_start(
-                base_sb[h][:], base[h * 2 * P : (h + 1) * 2 * P, :].rearrange("(a p) t -> p a t", p=P)
+                base_sb[h][:],
+                base.rearrange("(p a) t -> p a t", a=BLOCKS)[:, h * 2 : (h + 1) * 2, :],
             )
         offsets = held.tile([P, ENTRIES // 16], U16, name="offsets")
         nc.sync.dma_start(offsets[:], offs)
@@ -47,13 +48,13 @@ def tile_scatter_matmul_kernel(tc, base, x, w, b, offs, out):
         for e in range(EXPERTS):
             queues[e].dma_start(w_sb[e][:], w[e])
         bias_sb = held.tile([P, BLOCKS], F32, name="bias_sb")
-        with nc.allow_non_contiguous_dma(reason="one float32 bias value to a partition"):
-            nc.sync.dma_start(bias_sb[:], b.rearrange("(a p) o -> p (a o)", p=P))
+        nc.sync.dma_start(bias_sb[:], b.rearrange("(p a) o -> p (a o)", a=BLOCKS))
 
         scratch = held.tile([P, 1], F32, name="scratch")
         nc.vector.memset(scratch[:], 0.0)
         nc.scalar.activation(out=scratch[:], in_=scratch[:], func=mybir.ActivationFunctionType.Identity)
 
+        out_rows = out.rearrange("(p a) t -> p a t", a=BLOCKS)
         window = [windows.tile([P, TOKENS], F32, name="window%d" % a) for a in range(BLOCKS)]
         for a in range(BLOCKS):
             nc.tensor.matmul(window[a][:], ident[:], base_sb[a // 2][:, a % 2, :], start=True, stop=True)
@@ -62,7 +63,7 @@ def tile_scatter_matmul_kernel(tc, base, x, w, b, offs, out):
             for e in range(EXPERTS):
                 nc.tensor.matmul(
                     window[a][:].indirect(offsets[:, e * PIECE_COLS : (e + 1) * PIECE_COLS]),
-                    w_sb[e][:, a * P : (a + 1) * P],
+                    w_sb[e][:, a::BLOCKS],
                     x_sb[:, e * PIECE : (e + 1) * PIECE],
                     start=True,
                     stop=True,
@@ -73,10 +74,10 @@ def tile_scatter_matmul_kernel(tc, base, x, w, b, offs, out):
                     out=result[:], in0=window[a][:], scalar1=bias_sb[:, a : a + 1],
                     scalar2=None, op0=mybir.AluOpType.add,
                 )
-                nc.sync.dma_start(out[a * P : (a + 1) * P, :], result[:])
+                nc.sync.dma_start(out_rows[:, a, :], result[:])
             else:
                 nc.scalar.activation(
                     out=result[:], in_=window[a][:],
                     func=mybir.ActivationFunctionType.Identity, bias=bias_sb[:, a : a + 1],
                 )
-                nc.scalar.dma_start(out[a * P : (a + 1) * P, :], result[:])
+                nc.scalar.dma_start(out_rows[:, a, :], result[:])

@@ -33,20 +33,15 @@ def tile_scatter_matmul_kernel(tc, base, x, w, b, offs, out):
         ident = held.tile([P, P], BF16, name="ident")
         make_identity(nc, ident[:])
 
-        queues = [nc.sync, nc.scalar]
-        base_sb = [held.tile([P, 2, TOKENS], BF16, name="base_sb%d" % h) for h in range(2)]
-        for h in range(2):
-            queues[h].dma_start(
-                base_sb[h][:],
-                base.rearrange("(p a) t -> p a t", a=BLOCKS)[:, h * 2 : (h + 1) * 2, :],
-            )
+        base_sb = held.tile([P, BLOCKS, TOKENS], BF16, name="base_sb")
+        nc.sync.dma_start(base_sb[:], base.rearrange("(p a) t -> p a t", a=BLOCKS))
         offsets = held.tile([P, ENTRIES // 16], U16, name="offsets")
         nc.sync.dma_start(offsets[:], offs)
         x_sb = held.tile([P, ENTRIES], BF16, name="x_sb")
-        nc.scalar.dma_start(x_sb[:], x)
+        nc.sync.dma_start(x_sb[:], x)
         w_sb = [held.tile([P, FEATURES], BF16, name="w_sb%d" % e) for e in range(EXPERTS)]
         for e in range(EXPERTS):
-            queues[e].dma_start(w_sb[e][:], w[e])
+            nc.sync.dma_start(w_sb[e][:], w[e])
         bias_sb = held.tile([P, BLOCKS], F32, name="bias_sb")
         nc.sync.dma_start(bias_sb[:], b.rearrange("(p a) o -> p (a o)", a=BLOCKS))
 
@@ -57,7 +52,7 @@ def tile_scatter_matmul_kernel(tc, base, x, w, b, offs, out):
         out_rows = out.rearrange("(p a) t -> p a t", a=BLOCKS)
         window = [windows.tile([P, TOKENS], F32, name="window%d" % a) for a in range(BLOCKS)]
         for a in range(BLOCKS):
-            nc.tensor.matmul(window[a][:], ident[:], base_sb[a // 2][:, a % 2, :], start=True, stop=True)
+            nc.tensor.matmul(window[a][:], ident[:], base_sb[:, a, :], start=True, stop=True)
 
         for a in range(BLOCKS):
             for e in range(EXPERTS):

@@ -21,7 +21,7 @@ def tile_scatter_matmul_kernel(tc, base, x, w, b, offs, out):
     nc = tc.nc
     with (
         tc.tile_pool(name="held", bufs=1) as held,
-        tc.tile_pool(name="results", bufs=BLOCKS) as results,
+        tc.tile_pool(name="results", bufs=BLOCKS // 2) as results,
         tc.psum_pool(name="windows", bufs=1) as windows,
     ):
         zeros = held.tile([P, TOKENS], BF16, name="zeros")
@@ -63,16 +63,15 @@ def tile_scatter_matmul_kernel(tc, base, x, w, b, offs, out):
                     start=True,
                     stop=True,
                 )
-            result = results.tile([P, TOKENS], F32, name="result")
             if a % 2 == 0:
+                pair = results.tile([P, 2, TOKENS], F32, name="pair")
                 nc.vector.tensor_scalar(
-                    out=result[:], in0=window[a][:], scalar1=bias_sb[:, a : a + 1],
+                    out=pair[:, 0, :], in0=window[a][:], scalar1=bias_sb[:, a : a + 1],
                     scalar2=None, op0=mybir.AluOpType.add,
                 )
-                nc.sync.dma_start(out_rows[:, a, :], result[:])
             else:
                 nc.scalar.activation(
-                    out=result[:], in_=window[a][:],
+                    out=pair[:, 1, :], in_=window[a][:],
                     func=mybir.ActivationFunctionType.Identity, bias=bias_sb[:, a : a + 1],
                 )
-                nc.scalar.dma_start(out_rows[:, a, :], result[:])
+                nc.sync.dma_start(out_rows[:, a - 1 : a + 1, :], pair[:])

@@ -7,12 +7,14 @@ P = 128
 TOKENS = 256
 FEATURES = 512
 BLOCKS = FEATURES // P
+PAIR = 2
 EXPERTS = 2
 PIECE = 96
 ENTRIES = EXPERTS * PIECE
 PIECE_COLS = PIECE // 16
 
 WARM_MATMULS = 5
+WARM_ROWS = 32
 
 FLOPS = 2 * P * FEATURES * ENTRIES
 
@@ -21,14 +23,17 @@ def tile_scatter_matmul_kernel(tc, base, x, w, b, offs, out):
     nc = tc.nc
     with (
         tc.tile_pool(name="held", bufs=1) as held,
-        tc.tile_pool(name="results", bufs=BLOCKS // 2) as results,
+        tc.tile_pool(name="results", bufs=BLOCKS // PAIR) as results,
         tc.psum_pool(name="windows", bufs=1) as windows,
     ):
-        zeros = held.tile([P, TOKENS], BF16, name="zeros")
+        zeros = held.tile([P, WARM_ROWS], BF16, name="zeros")
         nc.gpsimd.memset(zeros[:], 0.0)
         idle_bank = windows.tile([P, TOKENS], F32, name="idle_bank")
         for i in range(WARM_MATMULS):
-            nc.tensor.matmul(idle_bank[:], zeros[:, 0:P], zeros[:], start=True, stop=True)
+            nc.tensor.matmul(
+                idle_bank[0:WARM_ROWS, :], zeros[:], zeros[:, 0:1].to_broadcast([P, TOKENS]),
+                start=True, stop=True,
+            )
 
         ident = held.tile([P, P], BF16, name="ident")
         make_identity(nc, ident[:])
@@ -54,24 +59,24 @@ def tile_scatter_matmul_kernel(tc, base, x, w, b, offs, out):
         for a in range(BLOCKS):
             nc.tensor.matmul(window[a][:], ident[:], base_sb[:, a, :], start=True, stop=True)
 
-        for a in range(BLOCKS):
+        for first in range(0, BLOCKS, PAIR):
+            pair = range(first, first + PAIR)
             for e in range(EXPERTS):
-                nc.tensor.matmul(
-                    window[a][:].indirect(offsets[:, e * PIECE_COLS : (e + 1) * PIECE_COLS]),
-                    w_sb[e][:, a::BLOCKS],
-                    x_sb[:, e * PIECE : (e + 1) * PIECE],
-                    start=True,
-                    stop=True,
-                )
-            if a % 2 == 0:
-                pair = results.tile([P, 2, TOKENS], F32, name="pair")
-                nc.vector.tensor_scalar(
-                    out=pair[:, 0, :], in0=window[a][:], scalar1=bias_sb[:, a : a + 1],
-                    scalar2=None, op0=mybir.AluOpType.add,
-                )
-            else:
-                nc.scalar.activation(
-                    out=pair[:, 1, :], in_=window[a][:],
-                    func=mybir.ActivationFunctionType.Identity, bias=bias_sb[:, a : a + 1],
-                )
-                nc.sync.dma_start(out_rows[:, a - 1 : a + 1, :], pair[:])
+                for a in pair:
+                    nc.tensor.matmul(
+                        window[a][:].indirect(offsets[:, e * PIECE_COLS : (e + 1) * PIECE_COLS]),
+                        w_sb[e][:, a::BLOCKS],
+                        x_sb[:, e * PIECE : (e + 1) * PIECE],
+                        start=True,
+                        stop=True,
+                    )
+            result = results.tile([P, PAIR, TOKENS], F32, name="result")
+            nc.vector.tensor_scalar(
+                out=result[:, 0, :], in0=window[first][:],
+                scalar1=bias_sb[:, first : first + 1], scalar2=None, op0=mybir.AluOpType.add,
+            )
+            nc.scalar.activation(
+                out=result[:, 1, :], in_=window[first + 1][:],
+                func=mybir.ActivationFunctionType.Identity, bias=bias_sb[:, first + 1 : first + 2],
+            )
+            nc.sync.dma_start(out_rows[:, first : first + PAIR, :], result[:])

import concourse.mybir as mybir
from concourse.masks import make_identity

BF16, F32, U16 = mybir.dt.bfloat16, mybir.dt.float32, mybir.dt.uint16

P = 128
TOKENS = 256
FEATURES = 512
BLOCKS = FEATURES // P
PAIR = 2
EXPERTS = 2
PIECE = 96
ENTRIES = EXPERTS * PIECE
PIECE_COLS = PIECE // 16

WARM_MATMULS = 5
WARM_ROWS = 32

FLOPS = 2 * P * FEATURES * ENTRIES


def tile_scatter_matmul_kernel(tc, base, x, w, b, offs, out):
    nc = tc.nc
    with (
        tc.tile_pool(name="held", bufs=1) as held,
        tc.tile_pool(name="results", bufs=BLOCKS // PAIR) as results,
        tc.psum_pool(name="windows", bufs=1) as windows,
    ):
        zeros = held.tile([P, WARM_ROWS], BF16, name="zeros")
        nc.gpsimd.memset(zeros[:], 0.0)
        idle_bank = windows.tile([P, TOKENS], F32, name="idle_bank")
        for i in range(WARM_MATMULS):
            nc.tensor.matmul(
                idle_bank[0:WARM_ROWS, :], zeros[:], zeros[:, 0:1].to_broadcast([P, TOKENS]),
                start=True, stop=True,
            )

        ident = held.tile([P, P], BF16, name="ident")
        make_identity(nc, ident[:])

        base_sb = held.tile([P, BLOCKS, TOKENS], BF16, name="base_sb")
        nc.sync.dma_start(base_sb[:], base.rearrange("(p a) t -> p a t", a=BLOCKS))
        offsets = held.tile([P, ENTRIES // 16], U16, name="offsets")
        nc.sync.dma_start(offsets[:], offs)
        x_sb = held.tile([P, ENTRIES], BF16, name="x_sb")
        nc.sync.dma_start(x_sb[:], x)
        w_sb = [held.tile([P, FEATURES], BF16, name="w_sb%d" % e) for e in range(EXPERTS)]
        for e in range(EXPERTS):
            nc.sync.dma_start(w_sb[e][:], w[e])
        bias_sb = held.tile([P, BLOCKS], F32, name="bias_sb")
        nc.sync.dma_start(bias_sb[:], b.rearrange("(p a) o -> p (a o)", a=BLOCKS))

        scratch = held.tile([P, 1], F32, name="scratch")
        nc.vector.memset(scratch[:], 0.0)
        nc.scalar.activation(out=scratch[:], in_=scratch[:], func=mybir.ActivationFunctionType.Identity)

        out_rows = out.rearrange("(p a) t -> p a t", a=BLOCKS)
        window = [windows.tile([P, TOKENS], F32, name="window%d" % a) for a in range(BLOCKS)]
        for a in range(BLOCKS):
            nc.tensor.matmul(window[a][:], ident[:], base_sb[:, a, :], start=True, stop=True)

        for first in range(0, BLOCKS, PAIR):
            pair = range(first, first + PAIR)
            for e in range(EXPERTS):
                for a in pair:
                    nc.tensor.matmul(
                        window[a][:].indirect(offsets[:, e * PIECE_COLS : (e + 1) * PIECE_COLS]),
                        w_sb[e][:, a::BLOCKS],
                        x_sb[:, e * PIECE : (e + 1) * PIECE],
                        start=True,
                        stop=True,
                    )
            result = results.tile([P, PAIR, TOKENS], F32, name="result")
            nc.vector.tensor_scalar(
                out=result[:, 0, :], in0=window[first][:],
                scalar1=bias_sb[:, first : first + 1], scalar2=None, op0=mybir.AluOpType.add,
            )
            nc.scalar.activation(
                out=result[:, 1, :], in_=window[first + 1][:],
                func=mybir.ActivationFunctionType.Identity, bias=bias_sb[:, first + 1 : first + 2],
            )
            nc.sync.dma_start(out_rows[:, first : first + PAIR, :], result[:])
